import numpy as np
import ml_dtypes


def mxq(x, axis, fmt="e4m3"):
    dtype, down = {"e4m3": (ml_dtypes.float8_e4m3fn, 7), "e5m2": (ml_dtypes.float8_e5m2, 14)}[fmt]
    v = np.moveaxis(np.asarray(x, np.float32).astype(ml_dtypes.bfloat16).astype(np.float64), axis, -1)
    blocks = v.reshape(v.shape[:-1] + (-1, 32))
    amax = np.abs(blocks).max(-1, keepdims=True)
    byte = np.maximum(np.where(amax > 0, np.frexp(amax)[1] - 1 + 127, 0) - down, 1)
    scale = np.exp2(byte - 127.0)
    codes = (blocks / scale).astype(np.float32).astype(dtype).astype(np.float64)
    return np.moveaxis((codes * scale).reshape(v.shape), -1, axis)


WIDE = False


def mx_kscale(k):
    if not WIDE:
        return np.ones(k)
    levels = np.array([10, -10, 5, -5, 0])
    if k % 512:
        return np.exp2(np.random.permutation(np.resize(levels, k // 32))).repeat(32)
    a = np.empty((k // 512, 16))
    for p in range(k // 512):
        a[p, :8] = np.random.permutation(np.resize(levels, 8))
        for g in range(8):
            far = levels[np.abs(levels - a[p, g]) >= 10]
            a[p, g + 8] = far[np.random.randint(len(far))]
    return np.exp2(a.ravel()).repeat(32)


def f64(x):
    return np.asarray(x).astype(np.float64)


def striped(idx):
    return np.tile(idx.reshape(-1, 16).T, (8, 1)).astype(np.uint16)


def unstriped(offs):
    return offs[:16].T.reshape(-1).astype(np.int64)


def pack_weight(w):
    k, n = w.shape
    w = f64(np.asarray(w, np.float32).astype(ml_dtypes.bfloat16)).reshape(k // 32, 32, n)
    amax = np.abs(w).max(1)
    byte = np.clip(np.where(amax > 0, np.frexp(amax)[1] - 1 + 127 - 7, 1), 1, 254)
    scaled = (w * np.exp2(127.0 - byte)[:, None, :]).reshape(k, n).astype(np.float32)
    words = np.ascontiguousarray(scaled.reshape(k // 512, 128, 4, n).transpose(0, 1, 3, 2)).astype(ml_dtypes.float8_e4m3fn).view(np.uint8)
    return words, np.ascontiguousarray(byte.astype(np.uint8).reshape(k // 512, 16, n))


def unpack_weight(words, scales):
    g, p, n, _ = words.shape
    vals = np.ascontiguousarray(words).view(ml_dtypes.float8_e4m3fn).astype(np.float64) * np.repeat(np.exp2(scales.astype(np.float64) - 127.0), 8, axis=1)[..., None]
    return vals.transpose(0, 1, 3, 2).reshape(g * 512, n)


K, T, D, S, V, R, N = 1024, 1024, 4, 512, 128, 8, 512


def setup_inputs():
    n = np.random.standard_normal
    s = mx_kscale(K)[:, None]
    packed = pack_weight(n((K, T)) * s)
    return {
        "x_words": packed[0],
        "x_scales": packed[1],
        "w": (n((D, K, N)) / np.sqrt(D * K) / s[None]).astype(np.float32),
        "offs": striped(np.concatenate([R * np.arange(V) + np.random.randint(0, R, V) for _ in range(D)])),
    }


def reference(x_words, x_scales, w, offs):
    idx = unstriped(offs)
    xq = unpack_weight(x_words, x_scales)[:, idx]
    wq = mxq(f64(w), 1, "e4m3")
    y = sum(wq[d].T @ xq[:, d * V:(d + 1) * V] for d in range(D))
    return y

@@ -1,0 +1,99 @@
+from contextlib import ExitStack
+
+import concourse.mybir as mybir
+
+K, T, TAPS, V, N = 1024, 1024, 4, 128, 512
+FLOPS = 2 * TAPS * K * N * V
+
+F32 = mybir.dt.float32
+BF16 = mybir.dt.bfloat16
+I32 = mybir.dt.int32
+U32 = mybir.dt.uint32
+U16 = mybir.dt.uint16
+U8 = mybir.dt.uint8
+FP8X4 = mybir.dt.float8_e4m3fn_x4
+
+P = 128
+PACK = 4
+K_PASS = P * PACK
+X_PASSES = K // K_PASS
+PASSES = TAPS * X_PASSES
+S = TAPS * V
+M_TILE = 128
+M_TILES = N // M_TILE
+HALF = N // 2
+
+
+def tile_picked_deform_lin_none_def_p_kernel(tc, x_words, x_scales, w, offs, out):
+    nc = tc.nc
+    with ExitStack() as ctx:
+        keep = ctx.enter_context(tc.tile_pool(name="keep", bufs=1))
+        psum = ctx.enter_context(tc.psum_pool(name="psum", bufs=1))
+
+        offsets = keep.tile([P, S // 16], U16, name="offsets")
+        nc.sync.dma_start(offsets[:], offs)
+
+        table_words = keep.tile([P, X_PASSES, T], U32, name="table_words", align_bytes=64)
+        nc.sync.dma_start(out=table_words[:].bitcast(I32), in_=x_words.rearrange("o p c r -> p o (c r)").bitcast(I32))
+
+        table_scales = keep.tile([P, T], U8, name="table_scales", align_bytes=64)
+        nc.gpsimd.memset(table_scales[:].bitcast(I32), 0)
+        for q in range(4):
+            nc.gpsimd.dma_start(
+                out=table_scales[32 * q : 32 * q + 4 * X_PASSES, :].bitcast(I32),
+                in_=x_scales[:, 4 * q : 4 * q + 4, :].bitcast(I32),
+            )
+
+        picked_words = []
+        for o in range(X_PASSES):
+            picked = keep.tile([P, S], U32, name="picked_words%d" % o, align_bytes=64)
+            nc.vector.tensor_copy(picked[:], table_words[:, o, :].indirect(offsets[:]))
+            picked_words.append(picked)
+        picked_scales = keep.tile([P, S], U8, name="picked_scales", align_bytes=64)
+        nc.vector.tensor_copy(picked_scales[:], table_scales[:].indirect(offsets[:]))
+
+        sums = [psum.tile([M_TILE, V], F32, name="sums%d" % t) for t in range(M_TILES)]
+
+        def load(g, c0, width):
+            d, o = divmod(g, X_PASSES)
+            raw = keep.tile([P, PACK, width], F32, name="raw%d_%d" % (g, c0), align_bytes=64)
+            rows = w[d, o * K_PASS : (o + 1) * K_PASS, c0 : c0 + width]
+            nc.sync.dma_start(out=raw[:], in_=rows.rearrange("(p j) m -> p j m", j=PACK))
+            return raw
+
+        def multiply(g, raw, raw_c0, c0, width, copy):
+            d, o = divmod(g, X_PASSES)
+            grouped = keep.tile([P, width, PACK], BF16, name="grouped%d_%d" % (g, c0), align_bytes=64)
+            copy(
+                grouped[:].rearrange("p (c i) j -> p c j i", i=4),
+                raw[:, :, c0 - raw_c0 : c0 - raw_c0 + width].rearrange("p j (c i) -> p c j i", i=4),
+            )
+            codes = keep.tile([P, width], U32, name="codes%d_%d" % (g, c0), align_bytes=64)
+            scales = keep.tile([P, width], U8, name="scales%d_%d" % (g, c0), align_bytes=64)
+            nc.vector.quantize_mx(out=codes[:].bitcast(FP8X4), scales=scales[:], in_=grouped[:].rearrange("p c j -> p (c j)"))
+            for m0 in range(0, width, M_TILE):
+                nc.tensor.matmul_mx(
+                    out=sums[(c0 + m0) // M_TILE][:],
+                    lhsT=codes[:, m0 : m0 + M_TILE].bitcast(FP8X4),
+                    lhsT_scale=scales[:, m0 : m0 + M_TILE],
+                    rhs=picked_words[o][:, d * V : (d + 1) * V].bitcast(FP8X4),
+                    rhs_scale=picked_scales[4 * o :, d * V : (d + 1) * V],
+                    start=(g == 0),
+                    stop=(g == PASSES - 1),
+                )
+
+        for g in range(PASSES - 1):
+            raw = load(g, 0, N)
+            multiply(g, raw, 0, 0, HALF, nc.vector.tensor_copy)
+            multiply(g, raw, 0, HALF, HALF, nc.scalar.copy)
+
+        last = PASSES - 1
+        for c0 in range(0, N, HALF):
+            raw = load(last, c0, HALF)
+            multiply(last, raw, c0, c0, M_TILE, nc.vector.tensor_copy)
+            multiply(last, raw, c0, c0 + M_TILE, M_TILE, nc.scalar.copy)
+            t0 = c0 // M_TILE
+            result = keep.tile([M_TILE, 2, V], F32, name="result%d" % c0, align_bytes=64)
+            nc.scalar.copy(result[:, 0, :], sums[t0][:])
+            nc.vector.tensor_copy(result[:, 1, :], sums[t0 + 1][:])
+            nc.sync.dma_start(out=out[c0 : c0 + HALF, :].rearrange("(t p) v -> p t v", p=M_TILE), in_=result[:])

@@ -30,16 +30,16 @@ def tile_picked_deform_lin_none_def_p_kernel(tc, x_words, x_scales, w, offs, out
         keep = ctx.enter_context(tc.tile_pool(name="keep", bufs=1))
         psum = ctx.enter_context(tc.psum_pool(name="psum", bufs=1))
 
-        offsets = keep.tile([P, S // 16], U16, name="offsets")
-        nc.sync.dma_start(offsets[:], offs)
-
         table_words = keep.tile([P, X_PASSES, T], U32, name="table_words", align_bytes=64)
         nc.sync.dma_start(out=table_words[:].bitcast(I32), in_=x_words.rearrange("o p c r -> p o (c r)").bitcast(I32))
 
+        offsets = keep.tile([P, S // 16], U16, name="offsets")
+        nc.sync.dma_start(offsets[:], offs)
+
         table_scales = keep.tile([P, T], U8, name="table_scales", align_bytes=64)
-        nc.gpsimd.memset(table_scales[:].bitcast(I32), 0)
+        nc.vector.memset(table_scales[:].bitcast(I32), 0)
         for q in range(4):
-            nc.gpsimd.dma_start(
+            nc.sync.dma_start(
                 out=table_scales[32 * q : 32 * q + 4 * X_PASSES, :].bitcast(I32),
                 in_=x_scales[:, 4 * q : 4 * q + 4, :].bitcast(I32),
             )

@@ -54,20 +54,23 @@ def tile_picked_deform_lin_none_def_p_kernel(tc, x_words, x_scales, w, offs, out
 
         sums = [psum.tile([M_TILE, V], F32, name="sums%d" % t) for t in range(M_TILES)]
 
-        def load(g, c0, width):
-            d, o = divmod(g, X_PASSES)
-            raw = keep.tile([P, PACK, width], F32, name="raw%d_%d" % (g, c0), align_bytes=64)
-            rows = w[d, o * K_PASS : (o + 1) * K_PASS, c0 : c0 + width]
-            nc.sync.dma_start(out=raw[:], in_=rows.rearrange("(p j) m -> p j m", j=PACK))
-            return raw
+        def load(g0, count, c0, width):
+            raw = keep.tile([P, count, PACK, width], F32, name="raw%d_%d" % (g0, c0), align_bytes=64)
+            rows = w.rearrange("d k m -> (d k) m")[g0 * K_PASS : (g0 + count) * K_PASS, c0 : c0 + width]
+            nc.sync.dma_start(out=raw[:], in_=rows.rearrange("(g p j) m -> p g j m", p=P, j=PACK))
+            return [raw[:, i] for i in range(count)]
 
-        def multiply(g, raw, raw_c0, c0, width, copy):
+        def multiply(g, raw, raw_c0, c0, shares):
             d, o = divmod(g, X_PASSES)
+            width = sum(share for share, copy in shares)
             grouped = keep.tile([P, width, PACK], BF16, name="grouped%d_%d" % (g, c0), align_bytes=64)
-            copy(
-                grouped[:].rearrange("p (c i) j -> p c j i", i=4),
-                raw[:, :, c0 - raw_c0 : c0 - raw_c0 + width].rearrange("p j (c i) -> p c j i", i=4),
-            )
+            at = 0
+            for share, copy in shares:
+                copy(
+                    grouped[:, at : at + share, :].rearrange("p (c i) j -> p c j i", i=4),
+                    raw[:, :, c0 - raw_c0 + at : c0 - raw_c0 + at + share].rearrange("p j (c i) -> p c j i", i=4),
+                )
+                at += share
             codes = keep.tile([P, width], U32, name="codes%d_%d" % (g, c0), align_bytes=64)
             scales = keep.tile([P, width], U8, name="scales%d_%d" % (g, c0), align_bytes=64)
             nc.vector.quantize_mx(out=codes[:].bitcast(FP8X4), scales=scales[:], in_=grouped[:].rearrange("p c j -> p (c j)"))
@@ -82,18 +85,24 @@ def tile_picked_deform_lin_none_def_p_kernel(tc, x_words, x_scales, w, offs, out
                     stop=(g == PASSES - 1),
                 )
 
-        for g in range(PASSES - 1):
-            raw = load(g, 0, N)
-            multiply(g, raw, 0, 0, HALF, nc.vector.tensor_copy)
-            multiply(g, raw, 0, HALF, HALF, nc.scalar.copy)
+        def store(t0, copies):
+            result = keep.tile([M_TILE, len(copies), V], F32, name="result%d" % t0, align_bytes=64)
+            for i, copy in enumerate(copies):
+                copy(result[:, i, :], sums[t0 + i][:])
+            rows = out[t0 * M_TILE : (t0 + len(copies)) * M_TILE, :]
+            nc.sync.dma_start(out=rows.rearrange("(t p) v -> p t v", p=M_TILE), in_=result[:])
 
+        on_vector, on_scalar = nc.vector.tensor_copy, nc.scalar.copy
         last = PASSES - 1
-        for c0 in range(0, N, HALF):
-            raw = load(last, c0, HALF)
-            multiply(last, raw, c0, c0, M_TILE, nc.vector.tensor_copy)
-            multiply(last, raw, c0, c0 + M_TILE, M_TILE, nc.scalar.copy)
-            t0 = c0 // M_TILE
-            result = keep.tile([M_TILE, 2, V], F32, name="result%d" % c0, align_bytes=64)
-            nc.scalar.copy(result[:, 0, :], sums[t0][:])
-            nc.vector.tensor_copy(result[:, 1, :], sums[t0 + 1][:])
-            nc.sync.dma_start(out=out[c0 : c0 + HALF, :].rearrange("(t p) v -> p t v", p=M_TILE), in_=result[:])
+        for g0, count in ((0, 3), (3, 2), (5, 1), (6, 1)):
+            for i, raw in enumerate(load(g0, count, 0, N)):
+                multiply(g0 + i, raw, 0, 0, [(HALF, on_vector)])
+                multiply(g0 + i, raw, 0, HALF, [(HALF, on_scalar)])
+        raw = load(last, 1, 0, HALF)[0]
+        multiply(last, raw, 0, 0, [(M_TILE, on_vector)])
+        multiply(last, raw, 0, M_TILE, [(M_TILE, on_scalar)])
+        store(0, [on_scalar, on_scalar])
+        for t in (2, 3):
+            raw = load(last, 1, t * M_TILE, M_TILE)[0]
+            multiply(last, raw, t * M_TILE, t * M_TILE, [(80, on_vector), (48, on_scalar)])
+            store(t, [on_scalar if t == 2 else on_vector])

@@ -104,5 +104,5 @@ def tile_picked_deform_lin_none_def_p_kernel(tc, x_words, x_scales, w, offs, out
         store(0, [on_scalar, on_scalar])
         for t in (2, 3):
             raw = load(last, 1, t * M_TILE, M_TILE)[0]
-            multiply(last, raw, t * M_TILE, t * M_TILE, [(80, on_vector), (48, on_scalar)])
+            multiply(last, raw, t * M_TILE, t * M_TILE, [(M_TILE, on_scalar if t == 2 else on_vector)])
             store(t, [on_scalar if t == 2 else on_vector])

@@ -36,12 +36,12 @@ def tile_picked_deform_lin_none_def_p_kernel(tc, x_words, x_scales, w, offs, out
         offsets = keep.tile([P, S // 16], U16, name="offsets")
         nc.sync.dma_start(offsets[:], offs)
 
-        table_scales = keep.tile([P, T], U8, name="table_scales", align_bytes=64)
+        table_scales = keep.tile([P, X_PASSES, T], U8, name="table_scales", align_bytes=64)
         nc.vector.memset(table_scales[:].bitcast(I32), 0)
-        for q in range(4):
+        for j in range(4):
             nc.sync.dma_start(
-                out=table_scales[32 * q : 32 * q + 4 * X_PASSES, :].bitcast(I32),
-                in_=x_scales[:, 4 * q : 4 * q + 4, :].bitcast(I32),
+                out=table_scales[j:P:32].bitcast(I32),
+                in_=x_scales[:, j:16:4, :].rearrange("o q c -> q o c").bitcast(I32),
             )
 
         picked_words = []
@@ -49,8 +49,11 @@ def tile_picked_deform_lin_none_def_p_kernel(tc, x_words, x_scales, w, offs, out
             picked = keep.tile([P, S], U32, name="picked_words%d" % o, align_bytes=64)
             nc.vector.tensor_copy(picked[:], table_words[:, o, :].indirect(offsets[:]))
             picked_words.append(picked)
-        picked_scales = keep.tile([P, S], U8, name="picked_scales", align_bytes=64)
-        nc.vector.tensor_copy(picked_scales[:], table_scales[:].indirect(offsets[:]))
+        picked_scales = []
+        for o in range(X_PASSES):
+            picked = keep.tile([P, S], U8, name="picked_scales%d" % o, align_bytes=64)
+            nc.vector.tensor_copy(picked[:], table_scales[:, o, :].indirect(offsets[:]))
+            picked_scales.append(picked)
 
         sums = [psum.tile([M_TILE, V], F32, name="sums%d" % t) for t in range(M_TILES)]
 
@@ -80,7 +83,7 @@ def tile_picked_deform_lin_none_def_p_kernel(tc, x_words, x_scales, w, offs, out
                     lhsT=codes[:, m0 : m0 + M_TILE].bitcast(FP8X4),
                     lhsT_scale=scales[:, m0 : m0 + M_TILE],
                     rhs=picked_words[o][:, d * V : (d + 1) * V].bitcast(FP8X4),
-                    rhs_scale=picked_scales[4 * o :, d * V : (d + 1) * V],
+                    rhs_scale=picked_scales[o][:, d * V : (d + 1) * V],
                     start=(g == 0),
                     stop=(g == PASSES - 1),
                 )

@@ -22,6 +22,7 @@ S = TAPS * V
 M_TILE = 128
 M_TILES = N // M_TILE
 HALF = N // 2
+HELD = range(2, 5)
 
 
 def tile_picked_deform_lin_none_def_p_kernel(tc, x_words, x_scales, w, offs, out):
@@ -63,8 +64,7 @@ def tile_picked_deform_lin_none_def_p_kernel(tc, x_words, x_scales, w, offs, out
             nc.sync.dma_start(out=raw[:], in_=rows.rearrange("(g p j) m -> p g j m", p=P, j=PACK))
             return [raw[:, i] for i in range(count)]
 
-        def multiply(g, raw, raw_c0, c0, shares):
-            d, o = divmod(g, X_PASSES)
+        def quantise(g, raw, raw_c0, c0, shares):
             width = sum(share for share, copy in shares)
             grouped = keep.tile([P, width, PACK], BF16, name="grouped%d_%d" % (g, c0), align_bytes=64)
             at = 0
@@ -77,6 +77,10 @@ def tile_picked_deform_lin_none_def_p_kernel(tc, x_words, x_scales, w, offs, out
             codes = keep.tile([P, width], U32, name="codes%d_%d" % (g, c0), align_bytes=64)
             scales = keep.tile([P, width], U8, name="scales%d_%d" % (g, c0), align_bytes=64)
             nc.vector.quantize_mx(out=codes[:].bitcast(FP8X4), scales=scales[:], in_=grouped[:].rearrange("p c j -> p (c j)"))
+            return g, c0, width, codes, scales
+
+        def multiply(g, c0, width, codes, scales):
+            d, o = divmod(g, X_PASSES)
             for m0 in range(0, width, M_TILE):
                 nc.tensor.matmul_mx(
                     out=sums[(c0 + m0) // M_TILE][:],
@@ -97,15 +101,21 @@ def tile_picked_deform_lin_none_def_p_kernel(tc, x_words, x_scales, w, offs, out
 
         on_vector, on_scalar = nc.vector.tensor_copy, nc.scalar.copy
         last = PASSES - 1
+        held = []
         for g0, count in ((0, 3), (3, 2), (5, 1), (6, 1)):
             for i, raw in enumerate(load(g0, count, 0, N)):
-                multiply(g0 + i, raw, 0, 0, [(HALF, on_vector)])
-                multiply(g0 + i, raw, 0, HALF, [(HALF, on_scalar)])
+                made = [quantise(g0 + i, raw, 0, 0, [(HALF, on_vector)]), quantise(g0 + i, raw, 0, HALF, [(HALF, on_scalar)])]
+                if g0 + i in HELD:
+                    held.extend(made)
+                else:
+                    for operands in made + held:
+                        multiply(*operands)
+                    held = []
         raw = load(last, 1, 0, HALF)[0]
-        multiply(last, raw, 0, 0, [(M_TILE, on_vector)])
-        multiply(last, raw, 0, M_TILE, [(M_TILE, on_scalar)])
+        multiply(*quantise(last, raw, 0, 0, [(M_TILE, on_vector)]))
+        multiply(*quantise(last, raw, 0, M_TILE, [(M_TILE, on_scalar)]))
         store(0, [on_scalar, on_scalar])
         for t in (2, 3):
             raw = load(last, 1, t * M_TILE, M_TILE)[0]
-            multiply(last, raw, t * M_TILE, t * M_TILE, [(M_TILE, on_scalar if t == 2 else on_vector)])
+            multiply(*quantise(last, raw, t * M_TILE, t * M_TILE, [(M_TILE, on_scalar if t == 2 else on_vector)]))
             store(t, [on_scalar if t == 2 else on_vector])

@@ -31,13 +31,13 @@ def tile_picked_deform_lin_none_def_p_kernel(tc, x_words, x_scales, w, offs, out
         keep = ctx.enter_context(tc.tile_pool(name="keep", bufs=1))
         psum = ctx.enter_context(tc.psum_pool(name="psum", bufs=1))
 
-        table_words = keep.tile([P, X_PASSES, T], U32, name="table_words", align_bytes=64)
+        table_words = keep.tile([P, X_PASSES, T], U32, name="table_words", align_bytes=256)
         nc.sync.dma_start(out=table_words[:].bitcast(I32), in_=x_words.rearrange("o p c r -> p o (c r)").bitcast(I32))
 
         offsets = keep.tile([P, S // 16], U16, name="offsets")
         nc.sync.dma_start(offsets[:], offs)
 
-        table_scales = keep.tile([P, X_PASSES, T], U8, name="table_scales", align_bytes=64)
+        table_scales = keep.tile([P, X_PASSES, T], U8, name="table_scales", align_bytes=256)
         nc.vector.memset(table_scales[:].bitcast(I32), 0)
         for j in range(4):
             nc.sync.dma_start(
@@ -47,26 +47,26 @@ def tile_picked_deform_lin_none_def_p_kernel(tc, x_words, x_scales, w, offs, out
 
         picked_words = []
         for o in range(X_PASSES):
-            picked = keep.tile([P, S], U32, name="picked_words%d" % o, align_bytes=64)
+            picked = keep.tile([P, S], U32, name="picked_words%d" % o, align_bytes=256)
             nc.vector.tensor_copy(picked[:], table_words[:, o, :].indirect(offsets[:]))
             picked_words.append(picked)
         picked_scales = []
         for o in range(X_PASSES):
-            picked = keep.tile([P, S], U8, name="picked_scales%d" % o, align_bytes=64)
+            picked = keep.tile([P, S], U8, name="picked_scales%d" % o, align_bytes=256)
             nc.vector.tensor_copy(picked[:], table_scales[:, o, :].indirect(offsets[:]))
             picked_scales.append(picked)
 
         sums = [psum.tile([M_TILE, V], F32, name="sums%d" % t) for t in range(M_TILES)]
 
         def load(g0, count, c0, width):
-            raw = keep.tile([P, count, PACK, width], F32, name="raw%d_%d" % (g0, c0), align_bytes=64)
+            raw = keep.tile([P, count, PACK, width], F32, name="raw%d_%d" % (g0, c0), align_bytes=256)
             rows = w.rearrange("d k m -> (d k) m")[g0 * K_PASS : (g0 + count) * K_PASS, c0 : c0 + width]
             nc.sync.dma_start(out=raw[:], in_=rows.rearrange("(g p j) m -> p g j m", p=P, j=PACK))
             return [raw[:, i] for i in range(count)]
 
         def quantise(g, raw, raw_c0, c0, shares):
             width = sum(share for share, copy in shares)
-            grouped = keep.tile([P, width, PACK], BF16, name="grouped%d_%d" % (g, c0), align_bytes=64)
+            grouped = keep.tile([P, width, PACK], BF16, name="grouped%d_%d" % (g, c0), align_bytes=256)
             at = 0
             for share, copy in shares:
                 copy(
@@ -74,8 +74,8 @@ def tile_picked_deform_lin_none_def_p_kernel(tc, x_words, x_scales, w, offs, out
                     raw[:, :, c0 - raw_c0 + at : c0 - raw_c0 + at + share].rearrange("p j (c i) -> p c j i", i=4),
                 )
                 at += share
-            codes = keep.tile([P, width], U32, name="codes%d_%d" % (g, c0), align_bytes=64)
-            scales = keep.tile([P, width], U8, name="scales%d_%d" % (g, c0), align_bytes=64)
+            codes = keep.tile([P, width], U32, name="codes%d_%d" % (g, c0), align_bytes=256)
+            scales = keep.tile([P, width], U8, name="scales%d_%d" % (g, c0), align_bytes=256)
             nc.vector.quantize_mx(out=codes[:].bitcast(FP8X4), scales=scales[:], in_=grouped[:].rearrange("p c j -> p (c j)"))
             return g, c0, width, codes, scales
 
@@ -93,7 +93,7 @@ def tile_picked_deform_lin_none_def_p_kernel(tc, x_words, x_scales, w, offs, out
                 )
 
         def store(t0, copies):
-            result = keep.tile([M_TILE, len(copies), V], F32, name="result%d" % t0, align_bytes=64)
+            result = keep.tile([M_TILE, len(copies), V], F32, name="result%d" % t0, align_bytes=256)
             for i, copy in enumerate(copies):
                 copy(result[:, i, :], sums[t0 + i][:])
             rows = out[t0 * M_TILE : (t0 + len(copies)) * M_TILE, :]

@@ -37,32 +37,33 @@ def tile_picked_deform_lin_none_def_p_kernel(tc, x_words, x_scales, w, offs, out
         offsets = keep.tile([P, S // 16], U16, name="offsets")
         nc.sync.dma_start(offsets[:], offs)
 
-        table_scales = keep.tile([P, X_PASSES, T], U8, name="table_scales", align_bytes=256)
-        nc.vector.memset(table_scales[:].bitcast(I32), 0)
-        for j in range(4):
-            nc.sync.dma_start(
-                out=table_scales[j:P:32].bitcast(I32),
-                in_=x_scales[:, j:16:4, :].rearrange("o q c -> q o c").bitcast(I32),
-            )
-
-        picked_words = []
-        for o in range(X_PASSES):
-            picked = keep.tile([P, S], U32, name="picked_words%d" % o, align_bytes=256)
-            nc.vector.tensor_copy(picked[:], table_words[:, o, :].indirect(offsets[:]))
-            picked_words.append(picked)
-        picked_scales = []
-        for o in range(X_PASSES):
-            picked = keep.tile([P, S], U8, name="picked_scales%d" % o, align_bytes=256)
-            nc.vector.tensor_copy(picked[:], table_scales[:, o, :].indirect(offsets[:]))
-            picked_scales.append(picked)
-
-        sums = [psum.tile([M_TILE, V], F32, name="sums%d" % t) for t in range(M_TILES)]
-
-        def load(g0, count, c0, width):
-            raw = keep.tile([P, count, PACK, width], F32, name="raw%d_%d" % (g0, c0), align_bytes=256)
+        def load(pool, g0, count, c0, width):
+            raw = pool.tile([P, count, PACK, width], F32, name="raw%d_%d" % (g0, c0), align_bytes=256)
             rows = w.rearrange("d k m -> (d k) m")[g0 * K_PASS : (g0 + count) * K_PASS, c0 : c0 + width]
             nc.sync.dma_start(out=raw[:], in_=rows.rearrange("(g p j) m -> p g j m", p=P, j=PACK))
             return [raw[:, i] for i in range(count)]
+
+        planes = keep.tile([P, X_PASSES, S], U8, name="planes", align_bytes=256)
+        with tc.tile_pool(name="early", bufs=1) as early:
+            table_scales = early.tile([P, X_PASSES, T], U8, name="table_scales", align_bytes=256)
+            nc.vector.memset(table_scales[:].bitcast(I32), 0)
+            nc.sync.dma_start(out=table_scales[0:P:8].bitcast(I32), in_=x_scales.rearrange("o r c -> r o c").bitcast(I32))
+            first = load(keep, 0, 3, 0, N)
+            spread = early.tile([P, X_PASSES, S], U8, name="spread", align_bytes=256)
+            for o in range(X_PASSES):
+                nc.vector.tensor_copy(spread[:, o, :], table_scales[:, o, :].indirect(offsets[:]))
+            nc.vector.tensor_copy(planes[:].bitcast(I32), spread[:].bitcast(I32))
+        for j in range(1, 4):
+            nc.sync.dma_start(out=planes[j:P:32].bitcast(I32), in_=planes[8 * j : P : 32].bitcast(I32))
+        late = ctx.enter_context(tc.tile_pool(name="late", bufs=1))
+
+        picked_words = []
+        for o in range(X_PASSES):
+            picked = late.tile([P, S], U32, name="picked_words%d" % o, align_bytes=256)
+            nc.vector.tensor_copy(picked[:], table_words[:, o, :].indirect(offsets[:]))
+            picked_words.append(picked)
+
+        sums = [psum.tile([M_TILE, V], F32, name="sums%d" % t) for t in range(M_TILES)]
 
         def quantise(g, raw, raw_c0, c0, shares):
             width = sum(share for share, copy in shares)
@@ -87,7 +88,7 @@ def tile_picked_deform_lin_none_def_p_kernel(tc, x_words, x_scales, w, offs, out
                     lhsT=codes[:, m0 : m0 + M_TILE].bitcast(FP8X4),
                     lhsT_scale=scales[:, m0 : m0 + M_TILE],
                     rhs=picked_words[o][:, d * V : (d + 1) * V].bitcast(FP8X4),
-                    rhs_scale=picked_scales[o][:, d * V : (d + 1) * V],
+                    rhs_scale=planes[:, o, d * V : (d + 1) * V],
                     start=(g == 0),
                     stop=(g == PASSES - 1),
                 )
@@ -103,7 +104,7 @@ def tile_picked_deform_lin_none_def_p_kernel(tc, x_words, x_scales, w, offs, out
         last = PASSES - 1
         held = []
         for g0, count in ((0, 3), (3, 2), (5, 1), (6, 1)):
-            for i, raw in enumerate(load(g0, count, 0, N)):
+            for i, raw in enumerate(first if g0 == 0 else load(late, g0, count, 0, N)):
                 made = [quantise(g0 + i, raw, 0, 0, [(HALF, on_vector)]), quantise(g0 + i, raw, 0, HALF, [(HALF, on_scalar)])]
                 if g0 + i in HELD:
                     held.extend(made)
@@ -111,11 +112,11 @@ def tile_picked_deform_lin_none_def_p_kernel(tc, x_words, x_scales, w, offs, out
                     for operands in made + held:
                         multiply(*operands)
                     held = []
-        raw = load(last, 1, 0, HALF)[0]
+        raw = load(late, last, 1, 0, HALF)[0]
         multiply(*quantise(last, raw, 0, 0, [(M_TILE, on_vector)]))
         multiply(*quantise(last, raw, 0, M_TILE, [(M_TILE, on_scalar)]))
         store(0, [on_scalar, on_scalar])
         for t in (2, 3):
-            raw = load(last, 1, t * M_TILE, M_TILE)[0]
+            raw = load(late, last, 1, t * M_TILE, M_TILE)[0]
             multiply(*quantise(last, raw, t * M_TILE, t * M_TILE, [(M_TILE, on_scalar if t == 2 else on_vector)]))
             store(t, [on_scalar if t == 2 else on_vector])

@@ -47,14 +47,15 @@ def tile_picked_deform_lin_none_def_p_kernel(tc, x_words, x_scales, w, offs, out
         with tc.tile_pool(name="early", bufs=1) as early:
             table_scales = early.tile([P, X_PASSES, T], U8, name="table_scales", align_bytes=256)
             nc.vector.memset(table_scales[:].bitcast(I32), 0)
-            nc.sync.dma_start(out=table_scales[0:P:8].bitcast(I32), in_=x_scales.rearrange("o r c -> r o c").bitcast(I32))
+            for j in range(2):
+                nc.sync.dma_start(out=table_scales[j:P:16].bitcast(I32), in_=x_scales[:, j:16:2, :].rearrange("o r c -> r o c").bitcast(I32))
             first = load(keep, 0, 3, 0, N)
             spread = early.tile([P, X_PASSES, S], U8, name="spread", align_bytes=256)
             for o in range(X_PASSES):
                 nc.vector.tensor_copy(spread[:, o, :], table_scales[:, o, :].indirect(offsets[:]))
             nc.vector.tensor_copy(planes[:].bitcast(I32), spread[:].bitcast(I32))
-        for j in range(1, 4):
-            nc.sync.dma_start(out=planes[j:P:32].bitcast(I32), in_=planes[8 * j : P : 32].bitcast(I32))
+        for j in range(2):
+            nc.sync.dma_start(out=planes[2 + j : P : 32].bitcast(I32), in_=planes[16 + j : P : 32].bitcast(I32))
         late = ctx.enter_context(tc.tile_pool(name="late", bufs=1))
 
         picked_words = []

from contextlib import ExitStack

import concourse.mybir as mybir

K, T, TAPS, V, N = 1024, 1024, 4, 128, 512
FLOPS = 2 * TAPS * K * N * V

F32 = mybir.dt.float32
BF16 = mybir.dt.bfloat16
I32 = mybir.dt.int32
U32 = mybir.dt.uint32
U16 = mybir.dt.uint16
U8 = mybir.dt.uint8
FP8X4 = mybir.dt.float8_e4m3fn_x4

P = 128
PACK = 4
K_PASS = P * PACK
X_PASSES = K // K_PASS
PASSES = TAPS * X_PASSES
S = TAPS * V
M_TILE = 128
M_TILES = N // M_TILE
HALF = N // 2
HELD = range(2, 5)


def tile_picked_deform_lin_none_def_p_kernel(tc, x_words, x_scales, w, offs, out):
    nc = tc.nc
    with ExitStack() as ctx:
        keep = ctx.enter_context(tc.tile_pool(name="keep", bufs=1))
        psum = ctx.enter_context(tc.psum_pool(name="psum", bufs=1))

        table_words = keep.tile([P, X_PASSES, T], U32, name="table_words", align_bytes=256)
        nc.sync.dma_start(out=table_words[:].bitcast(I32), in_=x_words.rearrange("o p c r -> p o (c r)").bitcast(I32))

        offsets = keep.tile([P, S // 16], U16, name="offsets")
        nc.sync.dma_start(offsets[:], offs)

        def load(pool, g0, count, c0, width):
            raw = pool.tile([P, count, PACK, width], F32, name="raw%d_%d" % (g0, c0), align_bytes=256)
            rows = w.rearrange("d k m -> (d k) m")[g0 * K_PASS : (g0 + count) * K_PASS, c0 : c0 + width]
            nc.sync.dma_start(out=raw[:], in_=rows.rearrange("(g p j) m -> p g j m", p=P, j=PACK))
            return [raw[:, i] for i in range(count)]

        planes = keep.tile([P, X_PASSES, S], U8, name="planes", align_bytes=256)
        with tc.tile_pool(name="early", bufs=1) as early:
            table_scales = early.tile([P, X_PASSES, T], U8, name="table_scales", align_bytes=256)
            nc.vector.memset(table_scales[:].bitcast(I32), 0)
            for j in range(2):
                nc.sync.dma_start(out=table_scales[j:P:16].bitcast(I32), in_=x_scales[:, j:16:2, :].rearrange("o r c -> r o c").bitcast(I32))
            first = load(keep, 0, 3, 0, N)
            spread = early.tile([P, X_PASSES, S], U8, name="spread", align_bytes=256)
            for o in range(X_PASSES):
                nc.vector.tensor_copy(spread[:, o, :], table_scales[:, o, :].indirect(offsets[:]))
            nc.vector.tensor_copy(planes[:].bitcast(I32), spread[:].bitcast(I32))
        for j in range(2):
            nc.sync.dma_start(out=planes[2 + j : P : 32].bitcast(I32), in_=planes[16 + j : P : 32].bitcast(I32))
        late = ctx.enter_context(tc.tile_pool(name="late", bufs=1))

        picked_words = []
        for o in range(X_PASSES):
            picked = late.tile([P, S], U32, name="picked_words%d" % o, align_bytes=256)
            nc.vector.tensor_copy(picked[:], table_words[:, o, :].indirect(offsets[:]))
            picked_words.append(picked)

        sums = [psum.tile([M_TILE, V], F32, name="sums%d" % t) for t in range(M_TILES)]

        def quantise(g, raw, raw_c0, c0, shares):
            width = sum(share for share, copy in shares)
            grouped = keep.tile([P, width, PACK], BF16, name="grouped%d_%d" % (g, c0), align_bytes=256)
            at = 0
            for share, copy in shares:
                copy(
                    grouped[:, at : at + share, :].rearrange("p (c i) j -> p c j i", i=4),
                    raw[:, :, c0 - raw_c0 + at : c0 - raw_c0 + at + share].rearrange("p j (c i) -> p c j i", i=4),
                )
                at += share
            codes = keep.tile([P, width], U32, name="codes%d_%d" % (g, c0), align_bytes=256)
            scales = keep.tile([P, width], U8, name="scales%d_%d" % (g, c0), align_bytes=256)
            nc.vector.quantize_mx(out=codes[:].bitcast(FP8X4), scales=scales[:], in_=grouped[:].rearrange("p c j -> p (c j)"))
            return g, c0, width, codes, scales

        def multiply(g, c0, width, codes, scales):
            d, o = divmod(g, X_PASSES)
            for m0 in range(0, width, M_TILE):
                nc.tensor.matmul_mx(
                    out=sums[(c0 + m0) // M_TILE][:],
                    lhsT=codes[:, m0 : m0 + M_TILE].bitcast(FP8X4),
                    lhsT_scale=scales[:, m0 : m0 + M_TILE],
                    rhs=picked_words[o][:, d * V : (d + 1) * V].bitcast(FP8X4),
                    rhs_scale=planes[:, o, d * V : (d + 1) * V],
                    start=(g == 0),
                    stop=(g == PASSES - 1),
                )

        def store(t0, copies):
            result = keep.tile([M_TILE, len(copies), V], F32, name="result%d" % t0, align_bytes=256)
            for i, copy in enumerate(copies):
                copy(result[:, i, :], sums[t0 + i][:])
            rows = out[t0 * M_TILE : (t0 + len(copies)) * M_TILE, :]
            nc.sync.dma_start(out=rows.rearrange("(t p) v -> p t v", p=M_TILE), in_=result[:])

        on_vector, on_scalar = nc.vector.tensor_copy, nc.scalar.copy
        last = PASSES - 1
        held = []
        for g0, count in ((0, 3), (3, 2), (5, 1), (6, 1)):
            for i, raw in enumerate(first if g0 == 0 else load(late, g0, count, 0, N)):
                made = [quantise(g0 + i, raw, 0, 0, [(HALF, on_vector)]), quantise(g0 + i, raw, 0, HALF, [(HALF, on_scalar)])]
                if g0 + i in HELD:
                    held.extend(made)
                else:
                    for operands in made + held:
                        multiply(*operands)
                    held = []
        raw = load(late, last, 1, 0, HALF)[0]
        multiply(*quantise(last, raw, 0, 0, [(M_TILE, on_vector)]))
        multiply(*quantise(last, raw, 0, M_TILE, [(M_TILE, on_scalar)]))
        store(0, [on_scalar, on_scalar])
        for t in (2, 3):
            raw = load(late, last, 1, t * M_TILE, M_TILE)[0]
            multiply(*quantise(last, raw, t * M_TILE, t * M_TILE, [(M_TILE, on_scalar if t == 2 else on_vector)]))
            store(t, [on_scalar if t == 2 else on_vector])
